import numpy as np, ml_dtypes
CORES = [19,147,275,403]
N = 4
import mx_ref
NC = 128
BF = ml_dtypes.bfloat16
def cut(t, i, w=512):
    return t[:, w * i:w * i + w]
def pk(c, s, i=0):
    return (np.ascontiguousarray(c[:, 512 * i:512 * i + 512]), mx_ref.live(s[:, 128 * i:128 * i + 128]))
def inputs(rng, e, E):
    def f(*shape):
        v = (rng.standard_normal(shape, dtype=np.float32) * np.exp2(rng.integers(-2, 3, shape[:-1] + (1,)))).astype(BF)
        return mx_ref.spread((v.astype(np.float32) * np.exp2(rng.integers(-E, E + 1, shape[:-2] + (1, 1))).astype(np.float32)).astype(BF), rng, e)
    def packed(k):
        c = np.zeros((N, 128, k * 512), np.uint8); s = np.zeros((N, 128, k * 128), np.uint8)
        for r in range(N):
            for i in range(k):
                a, b = mx_ref.quantize(f(128, 512)); c[r][:, 512 * i:512 * i + 512] = a; s[r][:, 128 * i:128 * i + 128] = mx_ref.plane(b, rng)
        return c, s
    d = {}
    d["wc"], d["ws"] = packed(N)
    d["x"] = f(N, 128, N * 4 * NC)
    return d
def setup_inputs(rng):
    return inputs(rng, 0, 0)
def setup_inputs_blocks(rng):
    return inputs(rng, 2, 0)
def setup_inputs_wide(rng):
    return inputs(rng, 0, 8)
def reference(wc, ws, x):
    y = np.zeros((N, 128, NC), np.float32)
    for r in range(N):
        for j in range(N):
            p = mx_ref.matmul(pk(wc[j], ws[j], r), mx_ref.quantize(cut(x[r], j, 4 * NC)))
            y[r] = p if j == 0 else y[r] + p
    return {"y": y}

from concourse.bass import DstId, RemoteDMATransfer
from concourse.mybir import dt

N = 4
TW = 128

SCRATCH = {
    "fc": ("dram", [128, TW], "float8_e4m3fn_x4"),
    "fp": ("dram", [128, TW], "uint8"),
    "rc": ("dram", [128, TW], "float8_e4m3fn_x4"),
    "rp": ("dram", [128, TW], "uint8"),
    "wq": ("sbuf", [128, N * TW], "float8_e4m3fn_x4"),
    "wp": ("sbuf", [128, N * TW], "uint8"),
    "lq": ("sbuf", [128, 3 * TW], "float8_e4m3fn_x4"),
    "lp": ("sbuf", [128, 3 * TW], "uint8"),
    "xb": ("sbuf", [128, N * 4 * TW], "bfloat16"),
    "xq": ("sbuf", [128, N * TW], "float8_e4m3fn_x4"),
    "xp": ("sbuf", [128, N * TW], "uint8"),
    "acc": ("psum", [128, 512], "float32"),
    "yb": ("sbuf", [128, TW], "float32"),
}
SEMAPHORES = ["ld_fp", "ld_fc", "ld_w", "ld_x", "quant", "at_rp", "at_rc", "in_via", "in_out", "in_far",
              "left", "mm", "copied", "stored"]


def _engines(mask):
    return [1 << i for i in range(mask.bit_length()) if (mask >> i) & 1]


def rank_program(g, core, T, topo):
    me = T.rank_of(core)
    if me is None:
        return
    S = T.sem
    u8 = dt.uint8
    others = [o for o in T.cores if o != core]
    far = [o for o in others if not topo.may_write(core, o)][0]
    via = [o for o in others if topo.same_plane(core, o)][0]
    out = [o for o in others if o != far and o != via][0]
    r_far, r_via, r_out = T.rank_of(far), T.rank_of(via), T.rank_of(out)

    def cols(i, w=TW):
        return slice(i * w, (i + 1) * w)

    g.sync.dma_start(T.fp[:], T.ws[:, cols(r_far)]).then_inc(S.ld_fp, 16)
    g.scalar.dma_start(T.fc[:].bitcast(u8), T.wc[:, cols(r_far, 4 * TW)]).then_inc(S.ld_fc, 16)
    g.sync.dma_start(T.wq[:].bitcast(u8), T.wc[:, :]).then_inc(S.ld_w, 16)
    g.scalar.dma_start(T.wp[:], T.ws[:, :]).then_inc(S.ld_w, 16)
    g.scalar.dma_start(T.xb[:], T.x[:, :]).then_inc(S.ld_x, 16)

    rid_v, pid_v = topo.addr(via, core)
    rid_o, pid_o = topo.addr(out, core)
    m_via, m_out = topo.mask(core, via), topo.mask(core, out)
    e_via, e_out = _engines(m_via), _engines(m_out)
    n_via, n_out = len(e_via), len(e_out)
    left = 0

    g.wait_ge(S.ld_fp, 16)
    g.remote_dma(T.rp[:], T.fp[:], S.at_rp, S.left, pid_v, rid_v, m_via)
    g.wait_ge(S.ld_fc, 16)
    g.remote_dma(T.rc[:].bitcast(u8), T.fc[:].bitcast(u8), S.at_rc, S.left, pid_v, rid_v, m_via)
    left += 2 * n_via

    both = _engines(m_via & m_out)
    h_via, h_out = sum(both[0::2]), sum(both[1::2])
    k = len(both) // 2
    g.wait_ge(S.ld_w, 32)
    g.remote_dma_fused([
        RemoteDMATransfer(dst_ids=[DstId(rid=rid_v, pnc=pid_v)], dma_engine_mask=h_via, remote_sem=S.in_via,
                          src=T.wq[:, cols(r_via)].bitcast(u8), dst=T.lq[:, cols(0)].bitcast(u8)),
        RemoteDMATransfer(dst_ids=[DstId(rid=rid_o, pnc=pid_o)], dma_engine_mask=h_out, remote_sem=S.in_out,
                          src=T.wq[:, cols(r_out)].bitcast(u8), dst=T.lq[:, cols(1)].bitcast(u8)),
    ], local_sem=S.left)
    g.remote_dma_fused([
        RemoteDMATransfer(dst_ids=[DstId(rid=rid_v, pnc=pid_v)], dma_engine_mask=h_via, remote_sem=S.in_via,
                          src=T.wp[:, cols(r_via)], dst=T.lp[:, cols(0)]),
        RemoteDMATransfer(dst_ids=[DstId(rid=rid_o, pnc=pid_o)], dma_engine_mask=h_out, remote_sem=S.in_out,
                          src=T.wp[:, cols(r_out)], dst=T.lp[:, cols(1)]),
    ], local_sem=S.left)
    left += 4 * k

    g.wait_ge(S.at_rp, n_via)
    g.remote_dma(T.lp[:, cols(2)], T.rp[:], S.in_far, S.left, pid_o, rid_o, m_out)
    g.wait_ge(S.at_rc, n_via)
    g.remote_dma(T.lq[:, cols(2)].bitcast(u8), T.rc[:].bitcast(u8), S.in_far, S.left, pid_o, rid_o, m_out)
    left += 2 * n_out
    g.wait_ge(S.left, left)

    g.vector.wait_ge(S.ld_x, 16)
    g.vector.quantize_mx(T.xq[:], T.xp[:], T.xb[:]).then_inc(S.quant, 1)

    acc = T.acc[:, 0:TW]
    g.tensor.wait_ge(S.ld_w, 32)
    g.tensor.wait_ge(S.quant, 1)
    g.tensor.matmul_mx(acc, T.wq[:, cols(me)], T.wp[:, cols(me)], T.xq[:, cols(me)], T.xp[:, cols(me)], True, False)
    g.tensor.wait_ge(S.in_via, 2 * k)
    g.tensor.matmul_mx(acc, T.lq[:, cols(0)], T.lp[:, cols(0)], T.xq[:, cols(r_via)], T.xp[:, cols(r_via)], False, False)
    g.tensor.wait_ge(S.in_out, 2 * k)
    g.tensor.matmul_mx(acc, T.lq[:, cols(1)], T.lp[:, cols(1)], T.xq[:, cols(r_out)], T.xp[:, cols(r_out)], False, False)
    g.tensor.wait_ge(S.in_far, 2 * n_out)
    g.tensor.matmul_mx(acc, T.lq[:, cols(2)], T.lp[:, cols(2)], T.xq[:, cols(r_far)], T.xp[:, cols(r_far)],
                       False, True).then_inc(S.mm, 1)

    g.vector.wait_ge(S.mm, 1)
    g.vector.tensor_copy(T.yb[:], acc).then_inc(S.copied, 1)
    g.sync.wait_ge(S.copied, 1)
    g.sync.dma_start(T.y[:, :], T.yb[:]).then_inc(S.stored, 16)
    g.sync.wait_ge(S.stored, 16)
